import numpy as np
import ml_dtypes


def mxq(x, axis, fmt="e4m3"):
    dtype, down = {"e4m3": (ml_dtypes.float8_e4m3fn, 7), "e5m2": (ml_dtypes.float8_e5m2, 14)}[fmt]
    v = np.moveaxis(np.asarray(x, np.float32).astype(ml_dtypes.bfloat16).astype(np.float64), axis, -1)
    blocks = v.reshape(v.shape[:-1] + (-1, 32))
    amax = np.abs(blocks).max(-1, keepdims=True)
    byte = np.maximum(np.where(amax > 0, np.frexp(amax)[1] - 1 + 127, 0) - down, 1)
    scale = np.exp2(byte - 127.0)
    codes = (blocks / scale).astype(np.float32).astype(dtype).astype(np.float64)
    return np.moveaxis((codes * scale).reshape(v.shape), -1, axis)


WIDE = False


def mx_kscale(k):
    if not WIDE:
        return np.ones(k)
    levels = np.array([10, -10, 5, -5, 0])
    if k % 512:
        return np.exp2(np.random.permutation(np.resize(levels, k // 32))).repeat(32)
    a = np.empty((k // 512, 16))
    for p in range(k // 512):
        a[p, :8] = np.random.permutation(np.resize(levels, 8))
        for g in range(8):
            far = levels[np.abs(levels - a[p, g]) >= 10]
            a[p, g + 8] = far[np.random.randint(len(far))]
    return np.exp2(a.ravel()).repeat(32)


def f64(x):
    return np.asarray(x).astype(np.float64)


def striped(idx):
    return np.tile(idx.reshape(-1, 16).T, (8, 1)).astype(np.uint16)


def unstriped(offs):
    return offs[:16].T.reshape(-1).astype(np.int64)


def striped8(idx):
    return np.concatenate([x.reshape(-1, 16).T for x in idx]).astype(np.uint16)


def runs(offs, k):
    lists = np.stack([offs[16 * r : 16 * r + 16].T.reshape(-1) for r in range(8)]).astype(np.int64)
    return lists[np.arange(k) % 512 // 64]


def pack_weight(w):
    k, n = w.shape
    w = f64(np.asarray(w, np.float32).astype(ml_dtypes.bfloat16)).reshape(k // 32, 32, n)
    amax = np.abs(w).max(1)
    byte = np.clip(np.where(amax > 0, np.frexp(amax)[1] - 1 + 127 - 7, 1), 1, 254)
    scaled = (w * np.exp2(127.0 - byte)[:, None, :]).reshape(k, n).astype(np.float32)
    words = np.ascontiguousarray(scaled.reshape(k // 512, 128, 4, n).transpose(0, 1, 3, 2)).astype(ml_dtypes.float8_e4m3fn).view(np.uint8)
    return words, np.ascontiguousarray(byte.astype(np.uint8).reshape(k // 512, 16, n))


def unpack_weight(words, scales):
    g, p, n, _ = words.shape
    vals = np.ascontiguousarray(words).view(ml_dtypes.float8_e4m3fn).astype(np.float64) * np.repeat(np.exp2(scales.astype(np.float64) - 127.0), 8, axis=1)[..., None]
    return vals.transpose(0, 1, 3, 2).reshape(g * 512, n)


def sigmoid(v):
    return 1.0 / (1.0 + np.exp(-np.maximum(v, -700.0)))


K, T, S, N, H, C = 512, 2048, 512, 512, 512, 512


def setup_inputs():
    n = np.random.standard_normal
    s = mx_kscale(K)[:, None]
    u = mx_kscale(S)
    packed_xT = pack_weight(n((K, T)) * s)
    return {
        "x_words": packed_xT[0],
        "x_scales": packed_xT[1],
        "w1": (n((K, H)) / np.sqrt(K) / s).astype(np.float32),
        "w2": (n((K, H)) / np.sqrt(K) / s).astype(np.float32),
        "tau": np.random.uniform(0.3, 0.9, (H, 1)).astype(np.float32),
        "tau2": np.random.uniform(0.3, 0.9, (H, 1)).astype(np.float32),
        "gn": (np.random.uniform(0.5, 1.5, (H, 1)) * u[:, None]).astype(np.float32),
        "w3": (n((H, N)) / np.sqrt(H) / u[:, None]).astype(np.float32),
        "gs": (np.random.uniform(0.5, 1.5, (K, 1)) / s).astype(np.float32),
        "sl": np.random.uniform(1.0, 2.0, (N, 1)).astype(np.float32),
        "th": (0.5 * n((N, 1))).astype(np.float32),
        "sl2": np.random.uniform(1.0, 2.0, (C, 1)).astype(np.float32),
        "th2": (0.5 * n((C, 1))).astype(np.float32),
        "offs": striped(np.random.permutation(T)[:S]),
        "two": striped(np.random.permutation(T)[:S]),
        "n1": striped8(np.stack([np.random.permutation(S) for _ in range(8)])),
        "n2": striped8(np.stack([np.random.permutation(S) for _ in range(8)])),
        "n3": striped(np.random.permutation(S)),
        "n4": striped(np.random.permutation(S)),
        "cand": striped(np.random.permutation(T)[:C]),
        "n5": striped(np.random.permutation(S)),
        "n6": striped(np.random.permutation(S)),
    }


def reference(x_words, x_scales, w1, w2, tau, tau2, gn, w3, gs, sl, th, sl2, th2, offs, two, n1, n2, n3, n4, cand, n5, n6):
    xq = unpack_weight(x_words, x_scales)[:, unstriped(offs)]
    y = mxq(f64(w1), 0, "e4m3").T @ xq
    st = np.maximum(y, y[np.arange(H)[:, None], runs(n1, H)])
    z = f64(gn) * (np.minimum(st, st[np.arange(H)[:, None], runs(n2, H)]))
    a = mxq(f64(w3), 0, "e4m3").T @ mxq(z, 0, "e4m3")
    sg = sigmoid(f64(sl) * (a[:, unstriped(n5)] - f64(th)))
    x_cand = unpack_weight(x_words, x_scales)[:, unstriped(cand)]
    x_two = unpack_weight(x_words, x_scales)[:, unstriped(two)]
    d = mxq(f64(w2), 0, "e4m3").T @ x_two
    top = d.max(axis=1, keepdims=True)
    ea = np.exp(f64(tau) * (d[:, unstriped(n3)] - top))
    ea2 = np.exp(f64(tau2) * (d[:, unstriped(n4)] - top))
    z2 = f64(gs) * (0.5 * d + np.log((ea + 0.25) / (ea2 + 0.25)))
    b = 0.0625 * ((x_cand.T @ mxq(z2, 0, "e4m3")))
    sg2 = sigmoid(f64(sl2) * (b[:, unstriped(n6)] - f64(th2)))
    return sg * b + sg2 * a

@@ -1,0 +1,251 @@
+from contextlib import ExitStack
+
+import concourse.mybir as mybir
+
+K, T, S, H = 512, 2048, 512, 512
+FLOPS = 4 * 2 * 512 * 512 * 512
+
+F32 = mybir.dt.float32
+BF16 = mybir.dt.bfloat16
+U32 = mybir.dt.uint32
+I32 = mybir.dt.int32
+U16 = mybir.dt.uint16
+U8 = mybir.dt.uint8
+FP8X4 = mybir.dt.float8_e4m3fn_x4
+ALU = mybir.AluOpType
+ACT = mybir.ActivationFunctionType
+
+P = 128
+PACK = 4
+HALF = S // 2
+LIST_COLS = S // 16
+
+
+def tile_picked_tfcdcxbhopmneos_none_p_kernel(
+    tc, x_words, x_scales, w1, w2, tau, tau2, gn, w3, gs, sl, th, sl2, th2,
+    offs, two, n1, n2, n3, n4, cand, n5, n6, out,
+):
+    nc = tc.nc
+    with ExitStack() as ctx:
+        keep = ctx.enter_context(tc.tile_pool(name="keep", bufs=1))
+        psum = ctx.enter_context(tc.psum_pool(name="psum", bufs=1))
+
+        def load_list(src, name):
+            tile = keep.tile([P, LIST_COLS], U16, name=name)
+            nc.sync.dma_start(tile[:], src)
+            return tile
+
+        def half_of(lst, h):
+            return lst[:, h * (LIST_COLS // 2) : (h + 1) * (LIST_COLS // 2)]
+
+        def cols(h):
+            return slice(h * HALF, (h + 1) * HALF)
+
+        def load_weight_half(w, h, name):
+            raw = keep.tile([P, PACK, HALF], F32, name=name)
+            nc.sync.dma_start(raw[:], w[:, cols(h)].rearrange("(p j) c -> p j c", j=PACK))
+            return raw
+
+        def load_vector(dst, src, pattern):
+            nc.gpsimd.dma_start(dst, src[:, 0].rearrange(pattern, t=PACK))
+
+        xs = keep.tile([P, T], U8, name="xs", align_bytes=64)
+        nc.vector.memset(xs[:].bitcast(I32), 0)
+        two_l = load_list(two, "two_l")
+        for q in range(4):
+            nc.scalar.dma_start(xs[32 * q : 32 * q + 4, :].bitcast(I32), x_scales[0, 4 * q : 4 * q + 4, :].bitcast(I32))
+        xw = keep.tile([P, T], U32, name="xw", align_bytes=64)
+        nc.sync.dma_start(xw[:].bitcast(I32), x_words[0].rearrange("p n t -> p (n t)").bitcast(I32))
+        w2_raw = [load_weight_half(w2, h, f"w2_raw{h}") for h in range(2)]
+        offs_l = load_list(offs, "offs_l")
+        cand_l = load_list(cand, "cand_l")
+        n3_l = load_list(n3, "n3_l")
+        n4_l = load_list(n4, "n4_l")
+        w1_raw = [load_weight_half(w1, h, f"w1_raw{h}") for h in range(2)]
+        n1_l = load_list(n1, "n1_l")
+        n2_l = load_list(n2, "n2_l")
+        w3_raw = [load_weight_half(w3, h, f"w3_raw{h}") for h in range(2)]
+        n5_l = load_list(n5, "n5_l")
+        n6_l = load_list(n6, "n6_l")
+
+        dealt = "(p t) -> p t"
+        plain = "(t p) -> p t"
+        rates = keep.tile([P, 2, 8], F32, name="rates")
+        load_vector(rates[:, 0, 0:PACK], tau, dealt)
+        load_vector(rates[:, 1, 0:PACK], tau2, dealt)
+        gn_t = keep.tile([P, PACK], F32, name="gn_t")
+        load_vector(gn_t[:], gn, dealt)
+        gs_t = keep.tile([P, PACK], F32, name="gs_t")
+        load_vector(gs_t[:], gs, dealt)
+        slopes = keep.tile([P, 2, 8], F32, name="slopes")
+        thresholds = keep.tile([P, 2, 8], F32, name="thresholds")
+        with nc.allow_non_contiguous_dma(reason="one value a row"):
+            load_vector(slopes[:, 0, 0:PACK], sl, plain)
+            load_vector(thresholds[:, 0, 0:PACK], th, plain)
+            load_vector(slopes[:, 1, 0:PACK], sl2, plain)
+            load_vector(thresholds[:, 1, 0:PACK], th2, plain)
+        quarter = keep.tile([P, 1], F32, name="quarter")
+        nc.vector.memset(quarter[:], 0.25)
+
+        def gather_scales(lst, name):
+            tile = keep.tile([P, S], U8, name=name, align_bytes=64)
+            nc.vector.tensor_copy(tile[:], xs[:].indirect(lst[:]))
+            return tile
+
+        def gather_words(lst, name):
+            tile = keep.tile([P, S], U32, name=name, align_bytes=64)
+            nc.vector.tensor_copy(tile[:], xw[:].indirect(lst[:]))
+            return tile
+
+        def quantize(grouped, name):
+            codes = keep.tile([P, S], U32, name=name + "_codes", align_bytes=64)
+            scales = keep.tile([P, S], U8, name=name + "_scales", align_bytes=64)
+            nc.vector.quantize_mx(out=codes[:].bitcast(FP8X4), scales=scales[:], in_=grouped[:])
+            return codes, scales
+
+        def product(tag, t, stat, mov):
+            bank = psum.tile([P, S], F32, name=f"{tag}{t}", tag=f"{tag}{t}")
+            m = slice(t * P, (t + 1) * P)
+            nc.tensor.matmul_mx(
+                out=bank[:], lhsT=stat[0][:, m].bitcast(FP8X4), lhsT_scale=stat[1][:, m],
+                rhs=mov[0][:].bitcast(FP8X4), rhs_scale=mov[1][:], start=True, stop=True,
+            )
+            return bank
+
+        def dealt_views(grouped, raw, h):
+            dst = grouped[:].rearrange("p (t m j) -> p m j t", t=PACK, j=PACK)[:, 64 * h : 64 * (h + 1)]
+            return dst, raw[:].rearrange("p j (m t) -> p m j t", t=PACK)
+
+        two_s = gather_scales(two_l, "two_s")
+        two_w = gather_words(two_l, "two_w")
+        w2_g = keep.tile([P, PACK * H], BF16, name="w2_g", align_bytes=64)
+        for h in range(2):
+            dst, src = dealt_views(w2_g, w2_raw[h], h)
+            nc.scalar.copy(dst, src)
+        offs_s = gather_scales(offs_l, "offs_s")
+        offs_w = gather_words(offs_l, "offs_w")
+        w2_q = quantize(w2_g, "w2")
+        d_bank = [product("first", t, w2_q, (two_w, two_s)) for t in range(PACK)]
+
+        w1_g = keep.tile([P, PACK * H], BF16, name="w1_g", align_bytes=64)
+        for h in range(2):
+            dst, src = dealt_views(w1_g, w1_raw[h], h)
+            nc.gpsimd.tensor_scalar(dst, src, 1.0, 0.0, ALU.mult, ALU.add)
+        w3_g = keep.tile([P, PACK * H], BF16, name="w3_g", align_bytes=64)
+        for h in range(2):
+            dst = w3_g[:].rearrange("p (c i j) -> p c j i", i=4, j=PACK)[:, 64 * h : 64 * (h + 1)]
+            nc.gpsimd.tensor_scalar(dst, w3_raw[h][:].rearrange("p j (c i) -> p c j i", i=4), 1.0, 0.0, ALU.mult, ALU.add)
+
+        top = keep.tile([P, PACK], F32, name="top")
+        exp_bias = keep.tile([P, PACK, 2], F32, name="exp_bias")
+        d_win = []
+        for t in range(PACK):
+            win = keep.tile([P, S], F32, name=f"d_win{t}")
+            nc.vector.tensor_scalar(win[:], d_bank[t][:], 1.0, None, ALU.mult, ALU.max, accum_out=top[:, t : t + 1])
+            nc.vector.tensor_scalar(exp_bias[:, t, :], rates[:, :, t], top[:, t : t + 1], -1.0, ALU.mult, ALU.mult)
+            d_win.append(win)
+
+        w1_q = quantize(w1_g, "w1")
+        y_bank = [product("second", t, w1_q, (offs_w, offs_s)) for t in range(PACK)]
+        cand_s = gather_scales(cand_l, "cand_s")
+        cand_w = gather_words(cand_l, "cand_w")
+
+        ea = keep.tile([P, 2, PACK, S], F32, name="ea")
+
+        def exps(t):
+            for k, lst in enumerate((n3_l, n4_l)):
+                for h in range(2):
+                    nc.scalar.activation(
+                        ea[:, k, t, cols(h)], d_win[t][:].indirect(half_of(lst, h)), ACT.Exp,
+                        bias=exp_bias[:, t, k : k + 1], scale=rates[:, k, t : t + 1],
+                    )
+
+        exps(0)
+        y_win = []
+        for t in range(PACK):
+            win = keep.tile([P, S], F32, name=f"y_win{t}")
+            nc.scalar.copy(win[:], y_bank[t][:])
+            y_win.append(win)
+        for t in range(1, PACK):
+            exps(t)
+        logs = keep.tile([P, 2, PACK, S], F32, name="logs")
+        for h in range(2):
+            nc.scalar.activation(
+                logs[:].rearrange("p k t s -> p (k t) s")[:, :, cols(h)],
+                ea[:].rearrange("p k t s -> p (k t) s")[:, :, cols(h)], ACT.Ln, bias=quarter[:],
+            )
+
+        def fetch(win, lst, name):
+            got = keep.tile([P, S], F32, name=name)
+            for h in range(2):
+                nc.vector.tensor_copy(got[:, cols(h)], win[:].indirect(half_of(lst, h)))
+            return got
+
+        def scale_and_group(planes, gain, name):
+            grouped = keep.tile([P, PACK * S], BF16, name=name, align_bytes=64)
+            for h in range(2):
+                dst = grouped[:].rearrange("p (c i t) -> p c t i", i=4, t=PACK)[:, 64 * h : 64 * (h + 1)]
+                src = planes[:, :, cols(h)].rearrange("p t (c i) -> p c t i", i=4)
+                nc.vector.tensor_tensor(dst, src, gain[:].unsqueeze(1).unsqueeze(3).to_broadcast([P, 64, PACK, 4]), ALU.mult)
+            return grouped
+
+        least = keep.tile([P, PACK, S], F32, name="least")
+        st_win = []
+        y_near = [None] * PACK
+        st_near = [None] * PACK
+        for step in range(PACK + 3):
+            if step < PACK:
+                y_near[step] = fetch(y_win[step], n1_l, f"y_near{step}")
+            if 1 <= step <= PACK:
+                t = step - 1
+                win = keep.tile([P, S], F32, name=f"st_win{t}")
+                nc.vector.tensor_tensor(win[:], y_bank[t][:], y_near[t][:], ALU.max)
+                st_win.append(win)
+            if step == 1:
+                w3_q = quantize(w3_g, "w3")
+            if 2 <= step <= PACK + 1:
+                t = step - 2
+                st_near[t] = fetch(st_win[t], n2_l, f"st_near{t}")
+            if 3 <= step:
+                t = step - 3
+                nc.vector.tensor_tensor(least[:, t, :], st_win[t][:], st_near[t][:], ALU.min)
+        sig_bias = keep.tile([P, 2, PACK], F32, name="sig_bias")
+        nc.vector.scalar_tensor_tensor(sig_bias[:], slopes[:, :, 0:PACK], -1.0, thresholds[:, :, 0:PACK], ALU.mult, ALU.mult)
+        z_g = scale_and_group(least, gn_t, "z_g")
+
+        ratio = keep.tile([P, PACK, S], F32, name="ratio")
+        nc.vector.tensor_tensor(ratio[:, :, cols(0)], logs[:, 0, :, cols(0)], logs[:, 1, :, cols(0)], ALU.subtract)
+        z_q = quantize(z_g, "z")
+        a_bank = [product("second", t, w3_q, z_q) for t in range(PACK)]
+        nc.vector.tensor_tensor(ratio[:, :, cols(1)], logs[:, 0, :, cols(1)], logs[:, 1, :, cols(1)], ALU.subtract)
+        mixed = keep.tile([P, PACK, S], F32, name="mixed")
+        for t in range(PACK):
+            nc.vector.scalar_tensor_tensor(mixed[:, t, :], d_bank[t][:], 0.5, ratio[:, t, :], ALU.mult, ALU.add)
+        z2_g = scale_and_group(mixed, gs_t, "z2_g")
+        z2_q = quantize(z2_g, "z2")
+        b_bank = [product("first", t, (cand_w, cand_s), z2_q) for t in range(PACK)]
+
+        def gate(win, lst, k, t, name):
+            got = keep.tile([P, S], F32, name=name)
+            for h in range(2):
+                nc.scalar.activation(
+                    got[:, cols(h)], win[:].indirect(half_of(lst, h)), ACT.Sigmoid,
+                    bias=sig_bias[:, k, t : t + 1], scale=slopes[:, k, t : t + 1],
+                )
+            return got
+
+        sg = []
+        for t in range(PACK):
+            win = keep.tile([P, S], F32, name=f"a_win{t}")
+            nc.scalar.copy(win[:], a_bank[t][:])
+            sg.append(gate(win, n5_l, 0, t, f"sg{t}"))
+        for t in range(PACK):
+            win = keep.tile([P, S], F32, name=f"b_win{t}")
+            nc.scalar.activation(win[:], b_bank[t][:], ACT.Copy, scale=0.0625)
+            sg2 = gate(win, n6_l, 1, t, f"sg2_{t}")
+            left = keep.tile([P, S], F32, name=f"left{t}")
+            nc.vector.scalar_tensor_tensor(left[:], b_bank[t][:], 0.0625, sg[t][:], ALU.mult, ALU.mult)
+            right = keep.tile([P, S], F32, name=f"right{t}")
+            nc.vector.tensor_tensor(right[:], a_bank[t][:], sg2[:], ALU.mult)
+            nc.vector.tensor_tensor(left[:], left[:], right[:], ALU.add)
+            nc.sync.dma_start(out[t * P : (t + 1) * P, :], left[:])

@@ -19,6 +19,9 @@ P = 128
 PACK = 4
 HALF = S // 2
 LIST_COLS = S // 16
+NEAR_ON_VECTOR = 1
+A_ON_VECTOR = 1
+B_ON_VECTOR = 3
 
 
 def tile_picked_tfcdcxbhopmneos_none_p_kernel(
@@ -41,42 +44,54 @@ def tile_picked_tfcdcxbhopmneos_none_p_kernel(
         def cols(h):
             return slice(h * HALF, (h + 1) * HALF)
 
-        def load_weight_half(w, h, name):
-            raw = keep.tile([P, PACK, HALF], F32, name=name)
-            nc.sync.dma_start(raw[:], w[:, cols(h)].rearrange("(p j) c -> p j c", j=PACK))
-            return raw
+        def window_with_weights(w, first, width, name):
+            win = keep.tile([P, S + PACK * width], F32, name=name)
+            raw = win[:, S:].rearrange("p (j c) -> p j c", j=PACK)
+            nc.sync.dma_start(raw, w[:, first : first + width].rearrange("(p j) c -> p j c", j=PACK))
+            return win, raw
 
         def load_vector(dst, src, pattern):
-            nc.gpsimd.dma_start(dst, src[:, 0].rearrange(pattern, t=PACK))
-
-        xs = keep.tile([P, T], U8, name="xs", align_bytes=64)
-        nc.vector.memset(xs[:].bitcast(I32), 0)
-        two_l = load_list(two, "two_l")
-        for q in range(4):
-            nc.scalar.dma_start(xs[32 * q : 32 * q + 4, :].bitcast(I32), x_scales[0, 4 * q : 4 * q + 4, :].bitcast(I32))
-        xw = keep.tile([P, T], U32, name="xw", align_bytes=64)
-        nc.sync.dma_start(xw[:].bitcast(I32), x_words[0].rearrange("p n t -> p (n t)").bitcast(I32))
-        w2_raw = [load_weight_half(w2, h, f"w2_raw{h}") for h in range(2)]
-        offs_l = load_list(offs, "offs_l")
-        cand_l = load_list(cand, "cand_l")
-        n3_l = load_list(n3, "n3_l")
-        n4_l = load_list(n4, "n4_l")
-        w1_raw = [load_weight_half(w1, h, f"w1_raw{h}") for h in range(2)]
-        n1_l = load_list(n1, "n1_l")
-        n2_l = load_list(n2, "n2_l")
-        w3_raw = [load_weight_half(w3, h, f"w3_raw{h}") for h in range(2)]
-        n5_l = load_list(n5, "n5_l")
-        n6_l = load_list(n6, "n6_l")
+            nc.sync.dma_start(dst, src[:, 0].rearrange(pattern, t=PACK))
 
         dealt = "(p t) -> p t"
         plain = "(t p) -> p t"
+        xs = keep.tile([P, T], U8, name="xs", align_bytes=64)
+        for q in range(4):
+            rows = x_scales[0, 4 * q : 4 * q + 4, :].bitcast(I32)
+            nc.sync.dma_start(xs[32 * q : 32 * q + 32, :].bitcast(I32), rows.unsqueeze(0).to_broadcast([8, 4, T // 4]))
+        offs_l = load_list(offs, "offs_l")
+        two_l = load_list(two, "two_l")
+        cand_l = load_list(cand, "cand_l")
+        y_win, w_raw = [], []
+        for h in range(2):
+            win, raw = window_with_weights(w1, h * HALF, HALF, f"y_win{h}")
+            y_win.append(win)
+            w_raw.append(raw)
+        xw = keep.tile([P, T], U32, name="xw", align_bytes=64)
+        nc.sync.dma_start(xw[:].bitcast(I32), x_words[0].rearrange("p n t -> p (n t)").bitcast(I32))
+        n1_l = load_list(n1, "n1_l")
+        for h in range(2):
+            win, raw = window_with_weights(w2, h * HALF, HALF, f"y_win{2 + h}")
+            y_win.append(win)
+            w_raw.append(raw)
+        w1_raw, w2_raw = w_raw[:2], w_raw[2:]
+        n2_l = load_list(n2, "n2_l")
         rates = keep.tile([P, 2, 8], F32, name="rates")
         load_vector(rates[:, 0, 0:PACK], tau, dealt)
         load_vector(rates[:, 1, 0:PACK], tau2, dealt)
+        n3_l = load_list(n3, "n3_l")
+        n4_l = load_list(n4, "n4_l")
+        d_win, w3_raw = [], []
+        for t in range(PACK):
+            win, raw = window_with_weights(w3, t * P, P, f"d_win{t}")
+            d_win.append(win)
+            w3_raw.append(raw)
         gn_t = keep.tile([P, PACK], F32, name="gn_t")
         load_vector(gn_t[:], gn, dealt)
         gs_t = keep.tile([P, PACK], F32, name="gs_t")
         load_vector(gs_t[:], gs, dealt)
+        n5_l = load_list(n5, "n5_l")
+        n6_l = load_list(n6, "n6_l")
         slopes = keep.tile([P, 2, 8], F32, name="slopes")
         thresholds = keep.tile([P, 2, 8], F32, name="thresholds")
         with nc.allow_non_contiguous_dma(reason="one value a row"):
@@ -113,61 +128,57 @@ def tile_picked_tfcdcxbhopmneos_none_p_kernel(
             return bank
 
         def dealt_views(grouped, raw, h):
-            dst = grouped[:].rearrange("p (t m j) -> p m j t", t=PACK, j=PACK)[:, 64 * h : 64 * (h + 1)]
-            return dst, raw[:].rearrange("p j (m t) -> p m j t", t=PACK)
+            dst = grouped[:].rearrange("p (v u m j) -> p v m j u", v=2, u=2, j=PACK)[:, :, 64 * h : 64 * (h + 1)]
+            return dst, raw.rearrange("p j (m v u) -> p v m j u", v=2, u=2)
 
-        two_s = gather_scales(two_l, "two_s")
-        two_w = gather_words(two_l, "two_w")
-        w2_g = keep.tile([P, PACK * H], BF16, name="w2_g", align_bytes=64)
-        for h in range(2):
-            dst, src = dealt_views(w2_g, w2_raw[h], h)
-            nc.scalar.copy(dst, src)
         offs_s = gather_scales(offs_l, "offs_s")
-        offs_w = gather_words(offs_l, "offs_w")
-        w2_q = quantize(w2_g, "w2")
-        d_bank = [product("first", t, w2_q, (two_w, two_s)) for t in range(PACK)]
-
+        two_s = gather_scales(two_l, "two_s")
+        cand_s = gather_scales(cand_l, "cand_s")
         w1_g = keep.tile([P, PACK * H], BF16, name="w1_g", align_bytes=64)
         for h in range(2):
-            dst, src = dealt_views(w1_g, w1_raw[h], h)
-            nc.gpsimd.tensor_scalar(dst, src, 1.0, 0.0, ALU.mult, ALU.add)
-        w3_g = keep.tile([P, PACK * H], BF16, name="w3_g", align_bytes=64)
+            nc.scalar.copy(*dealt_views(w1_g, w1_raw[h], h))
+        w1_q = quantize(w1_g, "w1")
+        offs_w = gather_words(offs_l, "offs_w")
+        y_bank = [product("second", t, w1_q, (offs_w, offs_s)) for t in range(PACK)]
+        two_w = gather_words(two_l, "two_w")
+        cand_w = gather_words(cand_l, "cand_w")
+
+        w2_g = keep.tile([P, PACK * H], BF16, name="w2_g", align_bytes=64)
         for h in range(2):
-            dst = w3_g[:].rearrange("p (c i j) -> p c j i", i=4, j=PACK)[:, 64 * h : 64 * (h + 1)]
-            nc.gpsimd.tensor_scalar(dst, w3_raw[h][:].rearrange("p j (c i) -> p c j i", i=4), 1.0, 0.0, ALU.mult, ALU.add)
+            nc.scalar.copy(*dealt_views(w2_g, w2_raw[h], h))
+        w2_q = quantize(w2_g, "w2")
+        d_bank = [product("first", t, w2_q, (two_w, two_s)) for t in range(PACK)]
+        w3_g = keep.tile([P, PACK * H], BF16, name="w3_g", align_bytes=64)
+        for t in range(PACK):
+            dst = w3_g[:].rearrange("p (c j) -> p c j", j=PACK)[:, t * P : (t + 1) * P]
+            nc.gpsimd.tensor_scalar(dst, w3_raw[t].rearrange("p j c -> p c j"), 1.0, 0.0, ALU.mult, ALU.add)
+
+        st_win = [keep.tile([P, 2 * S], F32, name=f"st_win{t}") for t in range(PACK)]
+        a_win = [keep.tile([P, 2 * S], F32, name=f"a_win{t}") for t in range(PACK)]
+        b_win = [keep.tile([P, 2 * S], F32, name=f"b_win{t}") for t in range(PACK)]
+        y_near = [win[:, S:] for win in st_win]
+        st_near = [win[:, S:] for win in a_win]
+        sg = [win[:, S:] for win in b_win]
+        for t in range(PACK):
+            nc.scalar.copy(y_win[t][:, :S], y_bank[t][:])
+            if t >= NEAR_ON_VECTOR:
+                nc.scalar.activation(y_near[t], y_win[t][:].indirect(n1_l[:]), ACT.Copy)
+            else:
+                nc.vector.tensor_copy(y_near[t], y_win[t][:].indirect(n1_l[:]))
 
         top = keep.tile([P, PACK], F32, name="top")
         exp_bias = keep.tile([P, PACK, 2], F32, name="exp_bias")
-        d_win = []
         for t in range(PACK):
-            win = keep.tile([P, S], F32, name=f"d_win{t}")
-            nc.vector.tensor_scalar(win[:], d_bank[t][:], 1.0, None, ALU.mult, ALU.max, accum_out=top[:, t : t + 1])
+            nc.vector.tensor_scalar(d_win[t][:, :S], d_bank[t][:], 1.0, None, ALU.mult, ALU.max, accum_out=top[:, t : t + 1])
             nc.vector.tensor_scalar(exp_bias[:, t, :], rates[:, :, t], top[:, t : t + 1], -1.0, ALU.mult, ALU.mult)
-            d_win.append(win)
-
-        w1_q = quantize(w1_g, "w1")
-        y_bank = [product("second", t, w1_q, (offs_w, offs_s)) for t in range(PACK)]
-        cand_s = gather_scales(cand_l, "cand_s")
-        cand_w = gather_words(cand_l, "cand_w")
 
         ea = keep.tile([P, 2, PACK, S], F32, name="ea")
-
-        def exps(t):
-            for k, lst in enumerate((n3_l, n4_l)):
-                for h in range(2):
-                    nc.scalar.activation(
-                        ea[:, k, t, cols(h)], d_win[t][:].indirect(half_of(lst, h)), ACT.Exp,
-                        bias=exp_bias[:, t, k : k + 1], scale=rates[:, k, t : t + 1],
-                    )
-
-        exps(0)
-        y_win = []
         for t in range(PACK):
-            win = keep.tile([P, S], F32, name=f"y_win{t}")
-            nc.scalar.copy(win[:], y_bank[t][:])
-            y_win.append(win)
-        for t in range(1, PACK):
-            exps(t)
+            for k, lst in enumerate((n3_l, n4_l)):
+                nc.scalar.activation(
+                    ea[:, k, t, :], d_win[t][:].indirect(lst[:]), ACT.Exp,
+                    bias=exp_bias[:, t, k : k + 1], scale=rates[:, k, t : t + 1],
+                )
         logs = keep.tile([P, 2, PACK, S], F32, name="logs")
         for h in range(2):
             nc.scalar.activation(
@@ -175,77 +186,87 @@ def tile_picked_tfcdcxbhopmneos_none_p_kernel(
                 ea[:].rearrange("p k t s -> p (k t) s")[:, :, cols(h)], ACT.Ln, bias=quarter[:],
             )
 
-        def fetch(win, lst, name):
-            got = keep.tile([P, S], F32, name=name)
-            for h in range(2):
-                nc.vector.tensor_copy(got[:, cols(h)], win[:].indirect(half_of(lst, h)))
-            return got
-
-        def scale_and_group(planes, gain, name):
-            grouped = keep.tile([P, PACK * S], BF16, name=name, align_bytes=64)
-            for h in range(2):
-                dst = grouped[:].rearrange("p (c i t) -> p c t i", i=4, t=PACK)[:, 64 * h : 64 * (h + 1)]
-                src = planes[:, :, cols(h)].rearrange("p t (c i) -> p c t i", i=4)
-                nc.vector.tensor_tensor(dst, src, gain[:].unsqueeze(1).unsqueeze(3).to_broadcast([P, 64, PACK, 4]), ALU.mult)
-            return grouped
+        def scale_and_group(grouped, planes, gain, h):
+            dst = grouped[:].rearrange("p (c i t) -> p c t i", i=2, t=PACK)[:, 128 * h : 128 * (h + 1)]
+            src = planes[:, :, cols(h)].rearrange("p t (c i) -> p c t i", i=2)
+            nc.vector.tensor_tensor(dst, src, gain[:].unsqueeze(1).unsqueeze(3).to_broadcast([P, 128, PACK, 2]), ALU.mult)
 
         least = keep.tile([P, PACK, S], F32, name="least")
-        st_win = []
-        y_near = [None] * PACK
-        st_near = [None] * PACK
-        for step in range(PACK + 3):
+        for step in range(PACK + 2):
             if step < PACK:
-                y_near[step] = fetch(y_win[step], n1_l, f"y_near{step}")
+                nc.vector.tensor_tensor(st_win[step][:, :S], y_bank[step][:], y_near[step], ALU.max)
+            if step == 0:
+                w3_q = quantize(w3_g, "w3")
             if 1 <= step <= PACK:
                 t = step - 1
-                win = keep.tile([P, S], F32, name=f"st_win{t}")
-                nc.vector.tensor_tensor(win[:], y_bank[t][:], y_near[t][:], ALU.max)
-                st_win.append(win)
-            if step == 1:
-                w3_q = quantize(w3_g, "w3")
-            if 2 <= step <= PACK + 1:
+                nc.vector.tensor_copy(st_near[t], st_win[t][:].indirect(n2_l[:]))
+            if 2 <= step:
                 t = step - 2
-                st_near[t] = fetch(st_win[t], n2_l, f"st_near{t}")
-            if 3 <= step:
-                t = step - 3
-                nc.vector.tensor_tensor(least[:, t, :], st_win[t][:], st_near[t][:], ALU.min)
+                nc.vector.tensor_tensor(least[:, t, :], st_win[t][:, :S], st_near[t], ALU.min)
         sig_bias = keep.tile([P, 2, PACK], F32, name="sig_bias")
         nc.vector.scalar_tensor_tensor(sig_bias[:], slopes[:, :, 0:PACK], -1.0, thresholds[:, :, 0:PACK], ALU.mult, ALU.mult)
-        z_g = scale_and_group(least, gn_t, "z_g")
-
-        ratio = keep.tile([P, PACK, S], F32, name="ratio")
-        nc.vector.tensor_tensor(ratio[:, :, cols(0)], logs[:, 0, :, cols(0)], logs[:, 1, :, cols(0)], ALU.subtract)
+        z_g = keep.tile([P, PACK * S], BF16, name="z_g", tag="z_then_ratio", align_bytes=64)
+        for h in range(2):
+            scale_and_group(z_g, least, gn_t, h)
         z_q = quantize(z_g, "z")
         a_bank = [product("second", t, w3_q, z_q) for t in range(PACK)]
-        nc.vector.tensor_tensor(ratio[:, :, cols(1)], logs[:, 0, :, cols(1)], logs[:, 1, :, cols(1)], ALU.subtract)
+
+        for t in range(A_ON_VECTOR):
+            nc.vector.tensor_copy(a_win[t][:, :S], a_bank[t][:])
+
+        ratio = keep.tile([P, PACK, S], F32, name="ratio", tag="z_then_ratio", align_bytes=64)
         mixed = keep.tile([P, PACK, S], F32, name="mixed")
-        for t in range(PACK):
-            nc.vector.scalar_tensor_tensor(mixed[:, t, :], d_bank[t][:], 0.5, ratio[:, t, :], ALU.mult, ALU.add)
-        z2_g = scale_and_group(mixed, gs_t, "z2_g")
-        z2_q = quantize(z2_g, "z2")
-        b_bank = [product("first", t, (cand_w, cand_s), z2_q) for t in range(PACK)]
+        z2_g = keep.tile([P, PACK * S], BF16, name="z2_g", align_bytes=64)
+        z2_codes = keep.tile([P, S], U32, name="z2_codes", align_bytes=64)
+        z2_scales = keep.tile([P, S], U8, name="z2_scales", align_bytes=64)
 
-        def gate(win, lst, k, t, name):
-            got = keep.tile([P, S], F32, name=name)
-            for h in range(2):
-                nc.scalar.activation(
-                    got[:, cols(h)], win[:].indirect(half_of(lst, h)), ACT.Sigmoid,
-                    bias=sig_bias[:, k, t : t + 1], scale=slopes[:, k, t : t + 1],
+        def subtract_logs(h):
+            nc.vector.tensor_tensor(ratio[:, :, cols(h)], logs[:, 0, :, cols(h)], logs[:, 1, :, cols(h)], ALU.subtract)
+
+        def mix(h):
+            for t in range(PACK):
+                nc.vector.scalar_tensor_tensor(
+                    mixed[:, t, cols(h)], d_bank[t][:, cols(h)], 0.5, ratio[:, t, cols(h)], ALU.mult, ALU.add
                 )
-            return got
 
-        sg = []
+        def quantize_half(h):
+            nc.vector.quantize_mx(
+                out=z2_codes[:, cols(h)].bitcast(FP8X4), scales=z2_scales[:, cols(h)],
+                in_=z2_g[:, PACK * h * HALF : PACK * (h + 1) * HALF],
+            )
+
+        subtract_logs(0)
+        mix(0)
+        scale_and_group(z2_g, mixed, gs_t, 0)
+        subtract_logs(1)
+        quantize_half(0)
+        mix(1)
+        scale_and_group(z2_g, mixed, gs_t, 1)
+        quantize_half(1)
+        b_bank = [product("first", t, (cand_w, cand_s), (z2_codes, z2_scales)) for t in range(PACK)]
+
+        def gate(got, win, lst, k, t):
+            nc.scalar.activation(
+                got, win[:].indirect(lst), ACT.Sigmoid, bias=sig_bias[:, k, t : t + 1], scale=slopes[:, k, t : t + 1]
+            )
+
         for t in range(PACK):
-            win = keep.tile([P, S], F32, name=f"a_win{t}")
-            nc.scalar.copy(win[:], a_bank[t][:])
-            sg.append(gate(win, n5_l, 0, t, f"sg{t}"))
+            if t >= A_ON_VECTOR:
+                nc.scalar.copy(a_win[t][:, :S], a_bank[t][:])
+            gate(sg[t], a_win[t], n5_l[:], 0, t)
+        for t in range(B_ON_VECTOR):
+            nc.vector.tensor_scalar(b_win[t][:, :S], b_bank[t][:], 0.0625, None, ALU.mult)
         for t in range(PACK):
-            win = keep.tile([P, S], F32, name=f"b_win{t}")
-            nc.scalar.activation(win[:], b_bank[t][:], ACT.Copy, scale=0.0625)
-            sg2 = gate(win, n6_l, 1, t, f"sg2_{t}")
+            last = t == PACK - 1
+            sg2 = keep.tile([P, S], F32, name=f"sg2_{t}")
             left = keep.tile([P, S], F32, name=f"left{t}")
-            nc.vector.scalar_tensor_tensor(left[:], b_bank[t][:], 0.0625, sg[t][:], ALU.mult, ALU.mult)
             right = keep.tile([P, S], F32, name=f"right{t}")
-            nc.vector.tensor_tensor(right[:], a_bank[t][:], sg2[:], ALU.mult)
-            nc.vector.tensor_tensor(left[:], left[:], right[:], ALU.add)
-            nc.sync.dma_start(out[t * P : (t + 1) * P, :], left[:])
+            if t >= B_ON_VECTOR:
+                nc.scalar.activation(b_win[t][:, :S], b_bank[t][:], ACT.Copy, scale=0.0625)
+            nc.vector.scalar_tensor_tensor(left[:], b_bank[t][:], 0.0625, sg[t], ALU.mult, ALU.mult)
+            for piece, lst in [(cols(h), half_of(n6_l, h)) for h in range(2)] if last else [(slice(0, S), n6_l[:])]:
+                gate(sg2[:, piece], b_win[t], lst, 1, t)
+                nc.vector.tensor_tensor(right[:, piece], a_bank[t][:, piece], sg2[:, piece], ALU.mult)
+                adder = nc.vector if last else nc.gpsimd
+                adder.tensor_tensor(left[:, piece], left[:, piece], right[:, piece], ALU.add)
+                nc.sync.dma_start(out[t * P : (t + 1) * P, piece], left[:, piece])

@@ -19,9 +19,10 @@ P = 128
 PACK = 4
 HALF = S // 2
 LIST_COLS = S // 16
-NEAR_ON_VECTOR = 1
-A_ON_VECTOR = 1
-B_ON_VECTOR = 3
+NEAR_ON_VECTOR = 2
+A_ON_VECTOR = 0
+B_ON_VECTOR = 4
+LEFT_ON_GPSIMD = 2
 
 
 def tile_picked_tfcdcxbhopmneos_none_p_kernel(
@@ -56,24 +57,21 @@ def tile_picked_tfcdcxbhopmneos_none_p_kernel(
         dealt = "(p t) -> p t"
         plain = "(t p) -> p t"
         xs = keep.tile([P, T], U8, name="xs", align_bytes=64)
+        nc.gpsimd.memset(xs[:].bitcast(I32), 0)
         for q in range(4):
-            rows = x_scales[0, 4 * q : 4 * q + 4, :].bitcast(I32)
-            nc.sync.dma_start(xs[32 * q : 32 * q + 32, :].bitcast(I32), rows.unsqueeze(0).to_broadcast([8, 4, T // 4]))
+            nc.sync.dma_start(xs[32 * q : 32 * q + 4, :].bitcast(I32), x_scales[0, 4 * q : 4 * q + 4, :].bitcast(I32))
         offs_l = load_list(offs, "offs_l")
         two_l = load_list(two, "two_l")
         cand_l = load_list(cand, "cand_l")
-        y_win, w_raw = [], []
-        for h in range(2):
-            win, raw = window_with_weights(w1, h * HALF, HALF, f"y_win{h}")
-            y_win.append(win)
-            w_raw.append(raw)
         xw = keep.tile([P, T], U32, name="xw", align_bytes=64)
         nc.sync.dma_start(xw[:].bitcast(I32), x_words[0].rearrange("p n t -> p (n t)").bitcast(I32))
-        n1_l = load_list(n1, "n1_l")
-        for h in range(2):
-            win, raw = window_with_weights(w2, h * HALF, HALF, f"y_win{2 + h}")
+        y_win, w_raw = [], []
+        for t in range(PACK):
+            win, raw = window_with_weights(w1 if t < 2 else w2, t % 2 * HALF, HALF, f"y_win{t}")
             y_win.append(win)
             w_raw.append(raw)
+            if t == 1:
+                n1_l = load_list(n1, "n1_l")
         w1_raw, w2_raw = w_raw[:2], w_raw[2:]
         n2_l = load_list(n2, "n2_l")
         rates = keep.tile([P, 2, 8], F32, name="rates")
@@ -100,31 +98,37 @@ def tile_picked_tfcdcxbhopmneos_none_p_kernel(
             load_vector(slopes[:, 1, 0:PACK], sl2, plain)
             load_vector(thresholds[:, 1, 0:PACK], th2, plain)
         quarter = keep.tile([P, 1], F32, name="quarter")
-        nc.vector.memset(quarter[:], 0.25)
+        nc.gpsimd.memset(quarter[:], 0.25)
 
-        def gather_scales(lst, name):
-            tile = keep.tile([P, S], U8, name=name, align_bytes=64)
+        def gather_scales(lst, name, tag=None):
+            tile = keep.tile([P, S], U8, name=name, tag=tag or name, align_bytes=64)
             nc.vector.tensor_copy(tile[:], xs[:].indirect(lst[:]))
             return tile
 
-        def gather_words(lst, name):
-            tile = keep.tile([P, S], U32, name=name, align_bytes=64)
+        def gather_words(lst, name, tag=None):
+            tile = keep.tile([P, S], U32, name=name, tag=tag or name, align_bytes=64)
             nc.vector.tensor_copy(tile[:], xw[:].indirect(lst[:]))
             return tile
 
-        def quantize(grouped, name):
-            codes = keep.tile([P, S], U32, name=name + "_codes", align_bytes=64)
+        def quantize(grouped, name, tag=None):
+            codes = keep.tile([P, S], U32, name=name + "_codes", tag=tag or name + "_codes", align_bytes=64)
             scales = keep.tile([P, S], U8, name=name + "_scales", align_bytes=64)
             nc.vector.quantize_mx(out=codes[:].bitcast(FP8X4), scales=scales[:], in_=grouped[:])
             return codes, scales
 
-        def product(tag, t, stat, mov):
-            bank = psum.tile([P, S], F32, name=f"{tag}{t}", tag=f"{tag}{t}")
+        def new_bank(tag, t):
+            return psum.tile([P, S], F32, name=f"{tag}{t}", tag=f"{tag}{t}")
+
+        def multiply(bank, t, stat, mov, piece):
             m = slice(t * P, (t + 1) * P)
             nc.tensor.matmul_mx(
-                out=bank[:], lhsT=stat[0][:, m].bitcast(FP8X4), lhsT_scale=stat[1][:, m],
-                rhs=mov[0][:].bitcast(FP8X4), rhs_scale=mov[1][:], start=True, stop=True,
+                out=bank[:, piece], lhsT=stat[0][:, m].bitcast(FP8X4), lhsT_scale=stat[1][:, m],
+                rhs=mov[0][:, piece].bitcast(FP8X4), rhs_scale=mov[1][:, piece], start=True, stop=True,
             )
+
+        def product(tag, t, stat, mov):
+            bank = new_bank(tag, t)
+            multiply(bank, t, stat, mov, slice(0, S))
             return bank
 
         def dealt_views(grouped, raw, h):
@@ -141,7 +145,7 @@ def tile_picked_tfcdcxbhopmneos_none_p_kernel(
         offs_w = gather_words(offs_l, "offs_w")
         y_bank = [product("second", t, w1_q, (offs_w, offs_s)) for t in range(PACK)]
         two_w = gather_words(two_l, "two_w")
-        cand_w = gather_words(cand_l, "cand_w")
+        cand_w = gather_words(cand_l, "cand_w", tag="w1_g")
 
         w2_g = keep.tile([P, PACK * H], BF16, name="w2_g", align_bytes=64)
         for h in range(2):
@@ -153,7 +157,7 @@ def tile_picked_tfcdcxbhopmneos_none_p_kernel(
             dst = w3_g[:].rearrange("p (c j) -> p c j", j=PACK)[:, t * P : (t + 1) * P]
             nc.gpsimd.tensor_scalar(dst, w3_raw[t].rearrange("p j c -> p c j"), 1.0, 0.0, ALU.mult, ALU.add)
 
-        st_win = [keep.tile([P, 2 * S], F32, name=f"st_win{t}") for t in range(PACK)]
+        st_win = [keep.tile([P, 2 * S], F32, name=f"st_win{t}", align_bytes=64) for t in range(PACK)]
         a_win = [keep.tile([P, 2 * S], F32, name=f"a_win{t}") for t in range(PACK)]
         b_win = [keep.tile([P, 2 * S], F32, name=f"b_win{t}") for t in range(PACK)]
         y_near = [win[:, S:] for win in st_win]
@@ -163,15 +167,17 @@ def tile_picked_tfcdcxbhopmneos_none_p_kernel(
             nc.scalar.copy(y_win[t][:, :S], y_bank[t][:])
             if t >= NEAR_ON_VECTOR:
                 nc.scalar.activation(y_near[t], y_win[t][:].indirect(n1_l[:]), ACT.Copy)
-            else:
+            elif t == 0:
                 nc.vector.tensor_copy(y_near[t], y_win[t][:].indirect(n1_l[:]))
 
         top = keep.tile([P, PACK], F32, name="top")
         exp_bias = keep.tile([P, PACK, 2], F32, name="exp_bias")
         for t in range(PACK):
             nc.vector.tensor_scalar(d_win[t][:, :S], d_bank[t][:], 1.0, None, ALU.mult, ALU.max, accum_out=top[:, t : t + 1])
-            nc.vector.tensor_scalar(exp_bias[:, t, :], rates[:, :, t], top[:, t : t + 1], -1.0, ALU.mult, ALU.mult)
+            nc.gpsimd.tensor_scalar(exp_bias[:, t, :], rates[:, :, t], top[:, t : t + 1], -1.0, ALU.mult, ALU.mult)
 
+        for t in range(1, NEAR_ON_VECTOR):
+            nc.vector.tensor_copy(y_near[t], y_win[t][:].indirect(n1_l[:]))
         ea = keep.tile([P, 2, PACK, S], F32, name="ea")
         for t in range(PACK):
             for k, lst in enumerate((n3_l, n4_l)):
@@ -186,64 +192,68 @@ def tile_picked_tfcdcxbhopmneos_none_p_kernel(
                 ea[:].rearrange("p k t s -> p (k t) s")[:, :, cols(h)], ACT.Ln, bias=quarter[:],
             )
 
-        def scale_and_group(grouped, planes, gain, h):
-            dst = grouped[:].rearrange("p (c i t) -> p c t i", i=2, t=PACK)[:, 128 * h : 128 * (h + 1)]
+        def scale_and_group(planes, gain, h, name):
+            grouped = keep.tile([P, PACK * HALF], BF16, name=name, align_bytes=64)
+            dst = grouped[:].rearrange("p (c i t) -> p c t i", i=2, t=PACK)
             src = planes[:, :, cols(h)].rearrange("p t (c i) -> p c t i", i=2)
             nc.vector.tensor_tensor(dst, src, gain[:].unsqueeze(1).unsqueeze(3).to_broadcast([P, 128, PACK, 2]), ALU.mult)
+            return grouped
+
+        def quantize_half(quantized, grouped, h):
+            codes, scales = quantized
+            nc.vector.quantize_mx(out=codes[:, cols(h)].bitcast(FP8X4), scales=scales[:, cols(h)], in_=grouped[:])
+
+        def operand_tiles(name):
+            codes = keep.tile([P, S], U32, name=name + "_codes", align_bytes=64)
+            scales = keep.tile([P, S], U8, name=name + "_scales", align_bytes=64)
+            return codes, scales
 
         least = keep.tile([P, PACK, S], F32, name="least")
         for step in range(PACK + 2):
             if step < PACK:
                 nc.vector.tensor_tensor(st_win[step][:, :S], y_bank[step][:], y_near[step], ALU.max)
-            if step == 0:
-                w3_q = quantize(w3_g, "w3")
             if 1 <= step <= PACK:
                 t = step - 1
                 nc.vector.tensor_copy(st_near[t], st_win[t][:].indirect(n2_l[:]))
             if 2 <= step:
                 t = step - 2
                 nc.vector.tensor_tensor(least[:, t, :], st_win[t][:, :S], st_near[t], ALU.min)
-        sig_bias = keep.tile([P, 2, PACK], F32, name="sig_bias")
-        nc.vector.scalar_tensor_tensor(sig_bias[:], slopes[:, :, 0:PACK], -1.0, thresholds[:, :, 0:PACK], ALU.mult, ALU.mult)
-        z_g = keep.tile([P, PACK * S], BF16, name="z_g", tag="z_then_ratio", align_bytes=64)
+        w3_q = quantize(w3_g, "w3", tag="st_win0")
+        sig_bias = keep.tile([P, 2, PACK], F32, name="sig_bias", tag="top")
+        nc.gpsimd.tensor_tensor(sig_bias[:], slopes[:, :, 0:PACK], thresholds[:, :, 0:PACK], ALU.mult)
+        nc.gpsimd.tensor_scalar(sig_bias[:], sig_bias[:], -1.0, 0.0, ALU.mult, ALU.add)
+        z_q = operand_tiles("z")
+        z_g = [scale_and_group(least, gn_t, h, f"z_g{h}") for h in range(2)]
         for h in range(2):
-            scale_and_group(z_g, least, gn_t, h)
-        z_q = quantize(z_g, "z")
+            quantize_half(z_q, z_g[h], h)
         a_bank = [product("second", t, w3_q, z_q) for t in range(PACK)]
-
         for t in range(A_ON_VECTOR):
             nc.vector.tensor_copy(a_win[t][:, :S], a_bank[t][:])
 
-        ratio = keep.tile([P, PACK, S], F32, name="ratio", tag="z_then_ratio", align_bytes=64)
         mixed = keep.tile([P, PACK, S], F32, name="mixed")
-        z2_g = keep.tile([P, PACK * S], BF16, name="z2_g", align_bytes=64)
-        z2_codes = keep.tile([P, S], U32, name="z2_codes", align_bytes=64)
-        z2_scales = keep.tile([P, S], U8, name="z2_scales", align_bytes=64)
+        z2_q = operand_tiles("z2")
 
         def subtract_logs(h):
-            nc.vector.tensor_tensor(ratio[:, :, cols(h)], logs[:, 0, :, cols(h)], logs[:, 1, :, cols(h)], ALU.subtract)
+            ratio = keep.tile([P, PACK, HALF], F32, name=f"ratio{h}", tag="z_g1", align_bytes=64)
+            nc.vector.tensor_tensor(ratio[:], logs[:, 0, :, cols(h)], logs[:, 1, :, cols(h)], ALU.subtract)
+            return ratio
 
-        def mix(h):
+        def mix(ratio, h):
             for t in range(PACK):
                 nc.vector.scalar_tensor_tensor(
-                    mixed[:, t, cols(h)], d_bank[t][:, cols(h)], 0.5, ratio[:, t, cols(h)], ALU.mult, ALU.add
+                    mixed[:, t, cols(h)], d_bank[t][:, cols(h)], 0.5, ratio[:, t, :], ALU.mult, ALU.add
                 )
 
-        def quantize_half(h):
-            nc.vector.quantize_mx(
-                out=z2_codes[:, cols(h)].bitcast(FP8X4), scales=z2_scales[:, cols(h)],
-                in_=z2_g[:, PACK * h * HALF : PACK * (h + 1) * HALF],
-            )
-
-        subtract_logs(0)
-        mix(0)
-        scale_and_group(z2_g, mixed, gs_t, 0)
-        subtract_logs(1)
-        quantize_half(0)
-        mix(1)
-        scale_and_group(z2_g, mixed, gs_t, 1)
-        quantize_half(1)
-        b_bank = [product("first", t, (cand_w, cand_s), (z2_codes, z2_scales)) for t in range(PACK)]
+        mix(subtract_logs(0), 0)
+        ratio = subtract_logs(1)
+        z2_first = scale_and_group(mixed, gs_t, 0, "z2_g0")
+        mix(ratio, 1)
+        quantize_half(z2_q, z2_first, 0)
+        quantize_half(z2_q, scale_and_group(mixed, gs_t, 1, "z2_g1"), 1)
+        b_bank = [new_bank("first", t) for t in range(PACK)]
+        for h in range(2):
+            for t in range(PACK):
+                multiply(b_bank[t], t, (cand_w, cand_s), z2_q, cols(h))
 
         def gate(got, win, lst, k, t):
             nc.scalar.activation(
@@ -263,7 +273,10 @@ def tile_picked_tfcdcxbhopmneos_none_p_kernel(
             right = keep.tile([P, S], F32, name=f"right{t}")
             if t >= B_ON_VECTOR:
                 nc.scalar.activation(b_win[t][:, :S], b_bank[t][:], ACT.Copy, scale=0.0625)
-            nc.vector.scalar_tensor_tensor(left[:], b_bank[t][:], 0.0625, sg[t], ALU.mult, ALU.mult)
+            if t < LEFT_ON_GPSIMD:
+                nc.gpsimd.tensor_tensor(left[:], b_win[t][:, :S], sg[t], ALU.mult)
+            else:
+                nc.vector.scalar_tensor_tensor(left[:], b_bank[t][:], 0.0625, sg[t], ALU.mult, ALU.mult)
             for piece, lst in [(cols(h), half_of(n6_l, h)) for h in range(2)] if last else [(slice(0, S), n6_l[:])]:
                 gate(sg2[:, piece], b_win[t], lst, 1, t)
                 nc.vector.tensor_tensor(right[:, piece], a_bank[t][:, piece], sg2[:, piece], ALU.mult)

@@ -22,7 +22,7 @@ LIST_COLS = S // 16
 NEAR_ON_VECTOR = 2
 A_ON_VECTOR = 0
 B_ON_VECTOR = 4
-LEFT_ON_GPSIMD = 2
+LEFT_ON_GPSIMD = 1
 
 
 def tile_picked_tfcdcxbhopmneos_none_p_kernel(
@@ -46,7 +46,7 @@ def tile_picked_tfcdcxbhopmneos_none_p_kernel(
             return slice(h * HALF, (h + 1) * HALF)
 
         def window_with_weights(w, first, width, name):
-            win = keep.tile([P, S + PACK * width], F32, name=name)
+            win = keep.tile([P, S + PACK * width], F32, name=name, align_bytes=64)
             raw = win[:, S:].rearrange("p (j c) -> p j c", j=PACK)
             nc.sync.dma_start(raw, w[:, first : first + width].rearrange("(p j) c -> p j c", j=PACK))
             return win, raw
@@ -152,10 +152,6 @@ def tile_picked_tfcdcxbhopmneos_none_p_kernel(
             nc.scalar.copy(*dealt_views(w2_g, w2_raw[h], h))
         w2_q = quantize(w2_g, "w2")
         d_bank = [product("first", t, w2_q, (two_w, two_s)) for t in range(PACK)]
-        w3_g = keep.tile([P, PACK * H], BF16, name="w3_g", align_bytes=64)
-        for t in range(PACK):
-            dst = w3_g[:].rearrange("p (c j) -> p c j", j=PACK)[:, t * P : (t + 1) * P]
-            nc.gpsimd.tensor_scalar(dst, w3_raw[t].rearrange("p j c -> p c j"), 1.0, 0.0, ALU.mult, ALU.add)
 
         st_win = [keep.tile([P, 2 * S], F32, name=f"st_win{t}", align_bytes=64) for t in range(PACK)]
         a_win = [keep.tile([P, 2 * S], F32, name=f"a_win{t}") for t in range(PACK)]
@@ -175,6 +171,11 @@ def tile_picked_tfcdcxbhopmneos_none_p_kernel(
         for t in range(PACK):
             nc.vector.tensor_scalar(d_win[t][:, :S], d_bank[t][:], 1.0, None, ALU.mult, ALU.max, accum_out=top[:, t : t + 1])
             nc.gpsimd.tensor_scalar(exp_bias[:, t, :], rates[:, :, t], top[:, t : t + 1], -1.0, ALU.mult, ALU.mult)
+
+        w3_g = keep.tile([P, PACK * H], BF16, name="w3_g", tag="y_win0", align_bytes=64)
+        for t in range(PACK):
+            dst = w3_g[:].rearrange("p (c j) -> p c j", j=PACK)[:, t * P : (t + 1) * P]
+            nc.gpsimd.tensor_scalar(dst, w3_raw[t].rearrange("p j c -> p c j"), 1.0, 0.0, ALU.mult, ALU.add)
 
         for t in range(1, NEAR_ON_VECTOR):
             nc.vector.tensor_copy(y_near[t], y_win[t][:].indirect(n1_l[:]))

@@ -195,9 +195,9 @@ def tile_picked_tfcdcxbhopmneos_none_p_kernel(
 
         def scale_and_group(planes, gain, h, name):
             grouped = keep.tile([P, PACK * HALF], BF16, name=name, align_bytes=64)
-            dst = grouped[:].rearrange("p (c i t) -> p c t i", i=2, t=PACK)
-            src = planes[:, :, cols(h)].rearrange("p t (c i) -> p c t i", i=2)
-            nc.vector.tensor_tensor(dst, src, gain[:].unsqueeze(1).unsqueeze(3).to_broadcast([P, 128, PACK, 2]), ALU.mult)
+            dst = grouped[:].rearrange("p (c i t) -> p c t i", i=4, t=PACK)
+            src = planes[:, :, cols(h)].rearrange("p t (c i) -> p c t i", i=4)
+            nc.vector.tensor_tensor(dst, src, gain[:].unsqueeze(1).unsqueeze(3).to_broadcast([P, 64, PACK, 4]), ALU.mult)
             return grouped
 
         def quantize_half(quantized, grouped, h):

from contextlib import ExitStack

import concourse.mybir as mybir

K, T, S, H = 512, 2048, 512, 512
FLOPS = 4 * 2 * 512 * 512 * 512

F32 = mybir.dt.float32
BF16 = mybir.dt.bfloat16
U32 = mybir.dt.uint32
I32 = mybir.dt.int32
U16 = mybir.dt.uint16
U8 = mybir.dt.uint8
FP8X4 = mybir.dt.float8_e4m3fn_x4
ALU = mybir.AluOpType
ACT = mybir.ActivationFunctionType

P = 128
PACK = 4
HALF = S // 2
LIST_COLS = S // 16
NEAR_ON_VECTOR = 2
A_ON_VECTOR = 0
B_ON_VECTOR = 4
LEFT_ON_GPSIMD = 1


def tile_picked_tfcdcxbhopmneos_none_p_kernel(
    tc, x_words, x_scales, w1, w2, tau, tau2, gn, w3, gs, sl, th, sl2, th2,
    offs, two, n1, n2, n3, n4, cand, n5, n6, out,
):
    nc = tc.nc
    with ExitStack() as ctx:
        keep = ctx.enter_context(tc.tile_pool(name="keep", bufs=1))
        psum = ctx.enter_context(tc.psum_pool(name="psum", bufs=1))

        def load_list(src, name):
            tile = keep.tile([P, LIST_COLS], U16, name=name)
            nc.sync.dma_start(tile[:], src)
            return tile

        def half_of(lst, h):
            return lst[:, h * (LIST_COLS // 2) : (h + 1) * (LIST_COLS // 2)]

        def cols(h):
            return slice(h * HALF, (h + 1) * HALF)

        def window_with_weights(w, first, width, name):
            win = keep.tile([P, S + PACK * width], F32, name=name, align_bytes=64)
            raw = win[:, S:].rearrange("p (j c) -> p j c", j=PACK)
            nc.sync.dma_start(raw, w[:, first : first + width].rearrange("(p j) c -> p j c", j=PACK))
            return win, raw

        def load_vector(dst, src, pattern):
            nc.sync.dma_start(dst, src[:, 0].rearrange(pattern, t=PACK))

        dealt = "(p t) -> p t"
        plain = "(t p) -> p t"
        xs = keep.tile([P, T], U8, name="xs", align_bytes=64)
        nc.gpsimd.memset(xs[:].bitcast(I32), 0)
        for q in range(4):
            nc.sync.dma_start(xs[32 * q : 32 * q + 4, :].bitcast(I32), x_scales[0, 4 * q : 4 * q + 4, :].bitcast(I32))
        offs_l = load_list(offs, "offs_l")
        two_l = load_list(two, "two_l")
        cand_l = load_list(cand, "cand_l")
        xw = keep.tile([P, T], U32, name="xw", align_bytes=64)
        nc.sync.dma_start(xw[:].bitcast(I32), x_words[0].rearrange("p n t -> p (n t)").bitcast(I32))
        y_win, w_raw = [], []
        for t in range(PACK):
            win, raw = window_with_weights(w1 if t < 2 else w2, t % 2 * HALF, HALF, f"y_win{t}")
            y_win.append(win)
            w_raw.append(raw)
            if t == 1:
                n1_l = load_list(n1, "n1_l")
        w1_raw, w2_raw = w_raw[:2], w_raw[2:]
        n2_l = load_list(n2, "n2_l")
        rates = keep.tile([P, 2, 8], F32, name="rates")
        load_vector(rates[:, 0, 0:PACK], tau, dealt)
        load_vector(rates[:, 1, 0:PACK], tau2, dealt)
        n3_l = load_list(n3, "n3_l")
        n4_l = load_list(n4, "n4_l")
        d_win, w3_raw = [], []
        for t in range(PACK):
            win, raw = window_with_weights(w3, t * P, P, f"d_win{t}")
            d_win.append(win)
            w3_raw.append(raw)
        gn_t = keep.tile([P, PACK], F32, name="gn_t")
        load_vector(gn_t[:], gn, dealt)
        gs_t = keep.tile([P, PACK], F32, name="gs_t")
        load_vector(gs_t[:], gs, dealt)
        n5_l = load_list(n5, "n5_l")
        n6_l = load_list(n6, "n6_l")
        slopes = keep.tile([P, 2, 8], F32, name="slopes")
        thresholds = keep.tile([P, 2, 8], F32, name="thresholds")
        with nc.allow_non_contiguous_dma(reason="one value a row"):
            load_vector(slopes[:, 0, 0:PACK], sl, plain)
            load_vector(thresholds[:, 0, 0:PACK], th, plain)
            load_vector(slopes[:, 1, 0:PACK], sl2, plain)
            load_vector(thresholds[:, 1, 0:PACK], th2, plain)
        quarter = keep.tile([P, 1], F32, name="quarter")
        nc.gpsimd.memset(quarter[:], 0.25)

        def gather_scales(lst, name, tag=None):
            tile = keep.tile([P, S], U8, name=name, tag=tag or name, align_bytes=64)
            nc.vector.tensor_copy(tile[:], xs[:].indirect(lst[:]))
            return tile

        def gather_words(lst, name, tag=None):
            tile = keep.tile([P, S], U32, name=name, tag=tag or name, align_bytes=64)
            nc.vector.tensor_copy(tile[:], xw[:].indirect(lst[:]))
            return tile

        def quantize(grouped, name, tag=None):
            codes = keep.tile([P, S], U32, name=name + "_codes", tag=tag or name + "_codes", align_bytes=64)
            scales = keep.tile([P, S], U8, name=name + "_scales", align_bytes=64)
            nc.vector.quantize_mx(out=codes[:].bitcast(FP8X4), scales=scales[:], in_=grouped[:])
            return codes, scales

        def new_bank(tag, t):
            return psum.tile([P, S], F32, name=f"{tag}{t}", tag=f"{tag}{t}")

        def multiply(bank, t, stat, mov, piece):
            m = slice(t * P, (t + 1) * P)
            nc.tensor.matmul_mx(
                out=bank[:, piece], lhsT=stat[0][:, m].bitcast(FP8X4), lhsT_scale=stat[1][:, m],
                rhs=mov[0][:, piece].bitcast(FP8X4), rhs_scale=mov[1][:, piece], start=True, stop=True,
            )

        def product(tag, t, stat, mov):
            bank = new_bank(tag, t)
            multiply(bank, t, stat, mov, slice(0, S))
            return bank

        def dealt_views(grouped, raw, h):
            dst = grouped[:].rearrange("p (v u m j) -> p v m j u", v=2, u=2, j=PACK)[:, :, 64 * h : 64 * (h + 1)]
            return dst, raw.rearrange("p j (m v u) -> p v m j u", v=2, u=2)

        offs_s = gather_scales(offs_l, "offs_s")
        two_s = gather_scales(two_l, "two_s")
        cand_s = gather_scales(cand_l, "cand_s")
        w1_g = keep.tile([P, PACK * H], BF16, name="w1_g", align_bytes=64)
        for h in range(2):
            nc.scalar.copy(*dealt_views(w1_g, w1_raw[h], h))
        w1_q = quantize(w1_g, "w1")
        offs_w = gather_words(offs_l, "offs_w")
        y_bank = [product("second", t, w1_q, (offs_w, offs_s)) for t in range(PACK)]
        two_w = gather_words(two_l, "two_w")
        cand_w = gather_words(cand_l, "cand_w", tag="w1_g")

        w2_g = keep.tile([P, PACK * H], BF16, name="w2_g", align_bytes=64)
        for h in range(2):
            nc.scalar.copy(*dealt_views(w2_g, w2_raw[h], h))
        w2_q = quantize(w2_g, "w2")
        d_bank = [product("first", t, w2_q, (two_w, two_s)) for t in range(PACK)]

        st_win = [keep.tile([P, 2 * S], F32, name=f"st_win{t}", align_bytes=64) for t in range(PACK)]
        a_win = [keep.tile([P, 2 * S], F32, name=f"a_win{t}") for t in range(PACK)]
        b_win = [keep.tile([P, 2 * S], F32, name=f"b_win{t}") for t in range(PACK)]
        y_near = [win[:, S:] for win in st_win]
        st_near = [win[:, S:] for win in a_win]
        sg = [win[:, S:] for win in b_win]
        for t in range(PACK):
            nc.scalar.copy(y_win[t][:, :S], y_bank[t][:])
            if t >= NEAR_ON_VECTOR:
                nc.scalar.activation(y_near[t], y_win[t][:].indirect(n1_l[:]), ACT.Copy)
            elif t == 0:
                nc.vector.tensor_copy(y_near[t], y_win[t][:].indirect(n1_l[:]))

        top = keep.tile([P, PACK], F32, name="top")
        exp_bias = keep.tile([P, PACK, 2], F32, name="exp_bias")
        for t in range(PACK):
            nc.vector.tensor_scalar(d_win[t][:, :S], d_bank[t][:], 1.0, None, ALU.mult, ALU.max, accum_out=top[:, t : t + 1])
            nc.gpsimd.tensor_scalar(exp_bias[:, t, :], rates[:, :, t], top[:, t : t + 1], -1.0, ALU.mult, ALU.mult)

        w3_g = keep.tile([P, PACK * H], BF16, name="w3_g", tag="y_win0", align_bytes=64)
        for t in range(PACK):
            dst = w3_g[:].rearrange("p (c j) -> p c j", j=PACK)[:, t * P : (t + 1) * P]
            nc.gpsimd.tensor_scalar(dst, w3_raw[t].rearrange("p j c -> p c j"), 1.0, 0.0, ALU.mult, ALU.add)

        for t in range(1, NEAR_ON_VECTOR):
            nc.vector.tensor_copy(y_near[t], y_win[t][:].indirect(n1_l[:]))
        ea = keep.tile([P, 2, PACK, S], F32, name="ea")
        for t in range(PACK):
            for k, lst in enumerate((n3_l, n4_l)):
                nc.scalar.activation(
                    ea[:, k, t, :], d_win[t][:].indirect(lst[:]), ACT.Exp,
                    bias=exp_bias[:, t, k : k + 1], scale=rates[:, k, t : t + 1],
                )
        logs = keep.tile([P, 2, PACK, S], F32, name="logs")
        for h in range(2):
            nc.scalar.activation(
                logs[:].rearrange("p k t s -> p (k t) s")[:, :, cols(h)],
                ea[:].rearrange("p k t s -> p (k t) s")[:, :, cols(h)], ACT.Ln, bias=quarter[:],
            )

        def scale_and_group(planes, gain, h, name):
            grouped = keep.tile([P, PACK * HALF], BF16, name=name, align_bytes=64)
            dst = grouped[:].rearrange("p (c i t) -> p c t i", i=4, t=PACK)
            src = planes[:, :, cols(h)].rearrange("p t (c i) -> p c t i", i=4)
            nc.vector.tensor_tensor(dst, src, gain[:].unsqueeze(1).unsqueeze(3).to_broadcast([P, 64, PACK, 4]), ALU.mult)
            return grouped

        def quantize_half(quantized, grouped, h):
            codes, scales = quantized
            nc.vector.quantize_mx(out=codes[:, cols(h)].bitcast(FP8X4), scales=scales[:, cols(h)], in_=grouped[:])

        def operand_tiles(name):
            codes = keep.tile([P, S], U32, name=name + "_codes", align_bytes=64)
            scales = keep.tile([P, S], U8, name=name + "_scales", align_bytes=64)
            return codes, scales

        least = keep.tile([P, PACK, S], F32, name="least")
        for step in range(PACK + 2):
            if step < PACK:
                nc.vector.tensor_tensor(st_win[step][:, :S], y_bank[step][:], y_near[step], ALU.max)
            if 1 <= step <= PACK:
                t = step - 1
                nc.vector.tensor_copy(st_near[t], st_win[t][:].indirect(n2_l[:]))
            if 2 <= step:
                t = step - 2
                nc.vector.tensor_tensor(least[:, t, :], st_win[t][:, :S], st_near[t], ALU.min)
        w3_q = quantize(w3_g, "w3", tag="st_win0")
        sig_bias = keep.tile([P, 2, PACK], F32, name="sig_bias", tag="top")
        nc.gpsimd.tensor_tensor(sig_bias[:], slopes[:, :, 0:PACK], thresholds[:, :, 0:PACK], ALU.mult)
        nc.gpsimd.tensor_scalar(sig_bias[:], sig_bias[:], -1.0, 0.0, ALU.mult, ALU.add)
        z_q = operand_tiles("z")
        z_g = [scale_and_group(least, gn_t, h, f"z_g{h}") for h in range(2)]
        for h in range(2):
            quantize_half(z_q, z_g[h], h)
        a_bank = [product("second", t, w3_q, z_q) for t in range(PACK)]
        for t in range(A_ON_VECTOR):
            nc.vector.tensor_copy(a_win[t][:, :S], a_bank[t][:])

        mixed = keep.tile([P, PACK, S], F32, name="mixed")
        z2_q = operand_tiles("z2")

        def subtract_logs(h):
            ratio = keep.tile([P, PACK, HALF], F32, name=f"ratio{h}", tag="z_g1", align_bytes=64)
            nc.vector.tensor_tensor(ratio[:], logs[:, 0, :, cols(h)], logs[:, 1, :, cols(h)], ALU.subtract)
            return ratio

        def mix(ratio, h):
            for t in range(PACK):
                nc.vector.scalar_tensor_tensor(
                    mixed[:, t, cols(h)], d_bank[t][:, cols(h)], 0.5, ratio[:, t, :], ALU.mult, ALU.add
                )

        mix(subtract_logs(0), 0)
        ratio = subtract_logs(1)
        z2_first = scale_and_group(mixed, gs_t, 0, "z2_g0")
        mix(ratio, 1)
        quantize_half(z2_q, z2_first, 0)
        quantize_half(z2_q, scale_and_group(mixed, gs_t, 1, "z2_g1"), 1)
        b_bank = [new_bank("first", t) for t in range(PACK)]
        for h in range(2):
            for t in range(PACK):
                multiply(b_bank[t], t, (cand_w, cand_s), z2_q, cols(h))

        def gate(got, win, lst, k, t):
            nc.scalar.activation(
                got, win[:].indirect(lst), ACT.Sigmoid, bias=sig_bias[:, k, t : t + 1], scale=slopes[:, k, t : t + 1]
            )

        for t in range(PACK):
            if t >= A_ON_VECTOR:
                nc.scalar.copy(a_win[t][:, :S], a_bank[t][:])
            gate(sg[t], a_win[t], n5_l[:], 0, t)
        for t in range(B_ON_VECTOR):
            nc.vector.tensor_scalar(b_win[t][:, :S], b_bank[t][:], 0.0625, None, ALU.mult)
        for t in range(PACK):
            last = t == PACK - 1
            sg2 = keep.tile([P, S], F32, name=f"sg2_{t}")
            left = keep.tile([P, S], F32, name=f"left{t}")
            right = keep.tile([P, S], F32, name=f"right{t}")
            if t >= B_ON_VECTOR:
                nc.scalar.activation(b_win[t][:, :S], b_bank[t][:], ACT.Copy, scale=0.0625)
            if t < LEFT_ON_GPSIMD:
                nc.gpsimd.tensor_tensor(left[:], b_win[t][:, :S], sg[t], ALU.mult)
            else:
                nc.vector.scalar_tensor_tensor(left[:], b_bank[t][:], 0.0625, sg[t], ALU.mult, ALU.mult)
            for piece, lst in [(cols(h), half_of(n6_l, h)) for h in range(2)] if last else [(slice(0, S), n6_l[:])]:
                gate(sg2[:, piece], b_win[t], lst, 1, t)
                nc.vector.tensor_tensor(right[:, piece], a_bank[t][:, piece], sg2[:, piece], ALU.mult)
                adder = nc.vector if last else nc.gpsimd
                adder.tensor_tensor(left[:, piece], left[:, piece], right[:, piece], ALU.add)
                nc.sync.dma_start(out[t * P : (t + 1) * P, piece], left[:, piece])
